import numpy as np
import ml_dtypes


def mxq(x, axis, fmt="e4m3"):
    dtype, down = {"e4m3": (ml_dtypes.float8_e4m3fn, 7), "e5m2": (ml_dtypes.float8_e5m2, 14)}[fmt]
    v = np.moveaxis(np.asarray(x, np.float32).astype(ml_dtypes.bfloat16).astype(np.float64), axis, -1)
    blocks = v.reshape(v.shape[:-1] + (-1, 32))
    amax = np.abs(blocks).max(-1, keepdims=True)
    byte = np.maximum(np.where(amax > 0, np.frexp(amax)[1] - 1 + 127, 0) - down, 1)
    scale = np.exp2(byte - 127.0)
    codes = (blocks / scale).astype(np.float32).astype(dtype).astype(np.float64)
    return np.moveaxis((codes * scale).reshape(v.shape), -1, axis)


WIDE = False


def mx_kscale(k):
    if not WIDE:
        return np.ones(k)
    levels = np.array([10, -10, 5, -5, 0])
    if k % 512:
        return np.exp2(np.random.permutation(np.resize(levels, k // 32))).repeat(32)
    a = np.empty((k // 512, 16))
    for p in range(k // 512):
        a[p, :8] = np.random.permutation(np.resize(levels, 8))
        for g in range(8):
            far = levels[np.abs(levels - a[p, g]) >= 10]
            a[p, g + 8] = far[np.random.randint(len(far))]
    return np.exp2(a.ravel()).repeat(32)


def f64(x):
    return np.asarray(x).astype(np.float64)


def striped(idx):
    return np.tile(np.asarray(idx).reshape(-1, 16).T, (8, 1)).astype(np.uint16)


def unstriped(offs):
    return offs[:16].T.reshape(-1).astype(np.int64)


E2M1 = np.array([0.0, 0.5, 1.0, 1.5, 2.0, 3.0, 4.0, 6.0, -0.0, -0.5, -1.0, -1.5, -2.0, -3.0, -4.0, -6.0])


def pack_weight(w, fmt):
    k, n = w.shape
    w = f64(np.asarray(w, np.float32).astype(ml_dtypes.bfloat16)).reshape(k // 32, 32, n)
    amax = np.abs(w).max(1)
    if fmt == "e4m3":
        byte = np.frexp(amax)[1] - 1 + 127 - 7
    else:
        mant, ex = np.frexp(amax / 6.0)
        byte = np.where(mant > 0.5, ex, ex - 1) + 127
    byte = np.clip(np.where(amax > 0, byte, 1), 1, 254)
    scaled = (w * np.exp2(127.0 - byte)[:, None, :]).reshape(k, n).astype(np.float32)
    by_word = np.ascontiguousarray(scaled.reshape(k // 512, 128, 4, n).transpose(0, 1, 3, 2))
    if fmt == "e4m3":
        words = by_word.astype(ml_dtypes.float8_e4m3fn).view(np.uint8)
    else:
        c = by_word.astype(ml_dtypes.float4_e2m1fn).view(np.uint8) & 0xF
        words = (c[..., 0::2] | (c[..., 1::2] << 4)).reshape(k // 512, 128, 2 * n)
    return np.ascontiguousarray(words), np.ascontiguousarray(byte.astype(np.uint8).reshape(k // 512, 16, n))


def unpack_weight(words, scales, fmt):
    g, _, n = scales.shape
    words = np.ascontiguousarray(words).reshape(g, 128, n, -1)
    if fmt == "e4m3":
        vals = words.view(ml_dtypes.float8_e4m3fn).astype(np.float64)
    else:
        nib = np.empty((g, 128, n, 4), np.uint8)
        nib[..., 0::2] = words & 0xF
        nib[..., 1::2] = words >> 4
        vals = E2M1[nib]
    vals = vals * np.repeat(np.exp2(scales.astype(np.float64) - 127.0), 8, axis=1)[..., None]
    return vals.transpose(0, 1, 3, 2).reshape(g * 512, n)


def sigmoid(v):
    return 1.0 / (1.0 + np.exp(-v))


D, E, T, I, Q, G = 512, 512, 2048, 512, 128, 32


def setup_inputs():
    n = np.random.standard_normal
    idx = np.random.permutation(T)[:I]
    fd = mx_kscale(D)
    fe = mx_kscale(E)
    keysp = pack_weight(n((D, T)) / fd[:, None], "e2m1")
    valsp = pack_weight(n((E, T)) / fe[:, None], "e2m1")
    return {
        "query": (n((D, Q)) * 0.5 / np.sqrt(D) * fd[:, None]).astype(np.float32),
        "keys_words": keysp[0],
        "keys_scales": keysp[1],
        "helpf": (np.random.uniform(0.5, 1.5, (Q, 1))).astype(np.float32),
        "gout": (n((E, Q)) * 1 / np.sqrt(E) * fe[:, None]).astype(np.float32),
        "vals_words": valsp[0],
        "vals_scales": valsp[1],
        "base": (0.5 * n((Q, I))).astype(np.float32),
        "offs": striped(idx),
    }


def reference(query, keys_words, keys_scales, helpf, gout, vals_words, vals_scales, base, offs):
    idx = unstriped(offs)
    keysu = unpack_weight(keys_words, keys_scales, "e2m1")
    valsu = unpack_weight(vals_words, vals_scales, "e2m1")
    queryq = mxq(f64(query), 0, "e4m3")
    keysidxg = keysu[:, idx]
    a = queryq.T @ keysidxg
    m1 = a.reshape(Q, G, I // G).mean(axis=2)
    gt = sigmoid(m1 * 4.0)
    gr = np.repeat(gt, I // G, axis=1)
    s = a * (gr * f64(helpf) + 1.0)
    p = np.exp(s - np.max(s, axis=1, keepdims=True))
    z = np.sum(p, axis=1, keepdims=True)
    goutq = mxq(f64(gout), 0, "e4m3")
    valsidxg = valsu[:, idx]
    c0 = goutq.T @ valsidxg
    dz = np.sum(c0 * p / np.square(z) * (-1.0), axis=1, keepdims=True)
    dp = c0 / z + dz
    ds = dp * p
    dgr = ds * a * f64(helpf)
    dgt = dgr.reshape(Q, G, I // G).sum(axis=2)
    dm1 = dgt * gt * (1.0 - gt) * 4.0
    e1 = dm1 / 16.0
    r1 = np.repeat(e1, I // G, axis=1)
    da = ds * (gr * f64(helpf) + 1.0) + r1
    hda = da * 512.0 * 2.0 * 512.0
    he1 = hda.reshape(Q, G, I // G).sum(axis=2)
    hdm1 = he1 / 16.0
    hdgt = hdm1 * 4.0 * (1.0 - gt) * gt
    r51 = np.repeat(hdgt, I // G, axis=1)
    hds = hda * (gr * f64(helpf) + 1.0) + r51 * f64(helpf) * a
    hdp = hds * p
    hdz = np.sum(hdp, axis=1, keepdims=True)
    hz = np.sum(hdp * c0 / np.square(z) * (-1.0), axis=1, keepdims=True) + np.sum(hdz * (-1.0) * c0 * p / np.square(np.square(z)) * (-1.0), axis=1, keepdims=True) * z * 2.0
    hp = hds * dp + hdz * (-1.0) / np.square(z) * c0 + hz
    hs = hp * p
    hgr = hda * ds * f64(helpf) + hs * a * f64(helpf)
    hgt = hdm1 * 4.0 * (1.0 - gt) * dgt + hgr.reshape(Q, G, I // G).sum(axis=2) - hdm1 * 4.0 * dgt * gt
    hm1 = hgt * gt * (1.0 - gt) * 4.0
    e52 = hm1 / 16.0
    r52 = np.repeat(e52, I // G, axis=1)
    ha = r51 * f64(helpf) * ds + hs * (gr * f64(helpf) + 1.0) + r52
    y = ha + f64(base)
    return y

@@ -1,0 +1,230 @@
+import math
+from contextlib import ExitStack
+
+import concourse.mybir as mybir
+
+D, T, SLOTS, Q = 512, 2048, 512, 128
+PAGES, PAGE = 32, 16
+FLOPS = 2 * 2 * D * Q * SLOTS
+P = 128
+PACK = 4
+HALVES = 2
+HS = SLOTS // HALVES
+HP = PAGES // HALVES
+PEN = 512.0 * 2.0 * 512.0
+
+F32 = mybir.dt.float32
+BF16 = mybir.dt.bfloat16
+I32 = mybir.dt.int32
+U32 = mybir.dt.uint32
+U16 = mybir.dt.uint16
+U8 = mybir.dt.uint8
+FP8X4 = mybir.dt.float8_e4m3fn_x4
+FP4X4 = mybir.dt.float4_e2m1fn_x4
+ALU = mybir.AluOpType
+ACT = mybir.ActivationFunctionType
+AX = mybir.AxisListType
+
+
+def tile_attend_gppagemates_kernel(tc, query, keys_words, keys_scales, helpf, gout, vals_words, vals_scales, base, offs, out):
+    nc = tc.nc
+    with ExitStack() as ctx:
+        sb = ctx.enter_context(tc.tile_pool(name="sb", bufs=1))
+        ps = ctx.enter_context(tc.psum_pool(name="ps", bufs=1))
+
+        def wide(name):
+            return sb.tile([P, SLOTS], F32, name=name, align_bytes=64)
+
+        def cols(h):
+            return slice(h * HS, (h + 1) * HS)
+
+        def pages(h):
+            return slice(h * HP, (h + 1) * HP)
+
+        def by_page(ap):
+            return ap.rearrange("p (g j) -> p g j", j=PAGE)
+
+        def spread(ap):
+            return ap.unsqueeze(2).to_broadcast([P, ap.shape[1], PAGE])
+
+        def load_scales(plane, scales):
+            for quad in range(4):
+                nc.sync.dma_start(out=plane[32 * quad : 32 * quad + 4, :].bitcast(I32), in_=scales[0, 4 * quad : 4 * quad + 4, :].bitcast(I32))
+
+        offsets = sb.tile([P, SLOTS // 16], U16, name="offsets")
+        k_words = sb.tile([P, T], U16, name="k_words", align_bytes=64)
+        v_words = sb.tile([P, T], U16, name="v_words", align_bytes=64)
+        k_plane = sb.tile([P, T], U8, name="k_plane", align_bytes=64)
+        v_plane = sb.tile([P, T], U8, name="v_plane", align_bytes=64)
+        q_raw = sb.tile([P, PACK, Q], F32, name="q_raw", align_bytes=64)
+        g_raw = sb.tile([P, PACK, Q], F32, name="g_raw", align_bytes=64)
+        help_col = sb.tile([P, 1], F32, name="help_col")
+        base_sb = wide("base_sb")
+
+        nc.vector.memset(k_plane[:].bitcast(I32), 0)
+        nc.vector.memset(v_plane[:].bitcast(I32), 0)
+        warm = sb.tile([P, 2], F32, name="warm")
+        nc.gpsimd.memset(warm[:, 0:1], 0.0)
+        warm2 = sb.tile([P, 2], F32, name="warm2")
+        nc.scalar.activation(warm2[:, 0:1], warm[:, 0:1], ACT.Exp)
+
+        nc.sync.dma_start(offsets[:], offs)
+        for h in range(HALVES):
+            nc.sync.dma_start(out=k_words[:].bitcast(I32)[:, h * 512 : (h + 1) * 512], in_=keys_words[0].bitcast(I32)[:, h * 512 : (h + 1) * 512])
+        nc.sync.dma_start(out=q_raw[:], in_=query.rearrange("(p j) w -> p j w", j=PACK))
+        nc.sync.dma_start(out=help_col[:], in_=helpf)
+        load_scales(k_plane, keys_scales)
+        nc.sync.dma_start(out=g_raw[:], in_=gout.rearrange("(p j) w -> p j w", j=PACK))
+        load_scales(v_plane, vals_scales)
+        nc.sync.dma_start(out=v_words[:].bitcast(I32), in_=vals_words[0].bitcast(I32))
+        nc.sync.dma_start(out=base_sb[:], in_=base)
+
+        hc = sb.tile([P, 4], F32, name="hc")
+        for j, (mul, add) in enumerate(((0.5, 0.0), (0.5, 1.0), (-1.0 / 16, 0.0), (1.0 / 16, 0.0))):
+            nc.gpsimd.tensor_scalar(hc[:, j : j + 1], help_col[:], mul, add, ALU.mult, ALU.add)
+
+        def cast(raw, name):
+            grouped = sb.tile([P, Q, PACK], BF16, name=name + "_bf", align_bytes=64)
+            nc.scalar.copy(grouped[:], raw[:].rearrange("p j w -> p w j"))
+            return grouped
+
+        def quantise(grouped, name):
+            codes = sb.tile([P, Q], U32, name=name + "_codes", align_bytes=64)
+            plane = sb.tile([P, Q], U8, name=name + "_plane", align_bytes=64)
+            nc.vector.quantize_mx(out=codes[:].bitcast(FP8X4), scales=plane[:], in_=grouped[:].rearrange("p w j -> p (w j)"))
+            return codes, plane
+
+        def gather(dst, window, h):
+            nc.vector.tensor_copy(dst[:, cols(h)], window[:].indirect(offsets[:, pages(h)]))
+
+        def product(dst, codes, plane, words, wplane, h):
+            nc.tensor.matmul_mx(out=dst, lhsT=codes[:].bitcast(FP8X4), lhsT_scale=plane[:], rhs=words[:, cols(h)].bitcast(FP4X4), rhs_scale=wplane[:, cols(h)], start=True, stop=True)
+
+        kg_words = sb.tile([P, SLOTS], U16, name="kg_words", align_bytes=64)
+        kg_plane = sb.tile([P, SLOTS], U8, name="kg_plane", align_bytes=64)
+        vg_words = sb.tile([P, SLOTS], U16, name="vg_words", align_bytes=64)
+        vg_plane = sb.tile([P, SLOTS], U8, name="vg_plane", align_bytes=64)
+        a_ps = [ps.tile([P, HS], F32, name="a_ps%d" % h) for h in range(HALVES)]
+        c_ps = ps.tile([P, SLOTS], F32, name="c_ps")
+
+        q_bf = cast(q_raw, "q")
+        gather(kg_words, k_words, 0)
+        gather(kg_words, k_words, 1)
+        gather(kg_plane, k_plane, 0)
+        q_codes, q_plane = quantise(q_bf, "q")
+        gather(kg_plane, k_plane, 1)
+        for h in range(HALVES):
+            product(a_ps[h][:], q_codes, q_plane, kg_words, kg_plane, h)
+
+        pg = sb.tile([P, 9, PAGES], F32, name="pg")
+        nn = sb.tile([P, 4, PAGES], F32, name="nn")
+        a_sum = sb.tile([P, PAGES], F32, name="a_sum")
+        th = sb.tile([P, PAGES], F32, name="th")
+        s = wide("s")
+        for h in range(HALVES):
+            nc.vector.tensor_reduce(a_sum[:, pages(h)], by_page(a_ps[h][:]), AX.X, ALU.add)
+        for h in range(HALVES):
+            nc.scalar.activation(th[:, pages(h)], a_sum[:, pages(h)], ACT.Tanh, scale=2.0 / PAGE)
+            nc.scalar.activation(pg[:, 8, pages(h)], th[:, pages(h)], ACT.Identity, scale=hc[:, 0:1], bias=hc[:, 1:2])
+        g_bf = cast(g_raw, "g")
+        gather(vg_plane, v_plane, 0)
+        gather(vg_plane, v_plane, 1)
+        for h in range(HALVES):
+            nc.vector.tensor_tensor(by_page(s[:, cols(h)]), by_page(a_ps[h][:]), spread(pg[:, 8, pages(h)]), ALU.mult)
+        g_codes, g_plane = quantise(g_bf, "g")
+        gather(vg_words, v_words, 0)
+        neg_max = sb.tile([P, 1], F32, name="neg_max")
+        nc.vector.tensor_reduce(neg_max[:], s[:], AX.X, ALU.max, negate=True)
+        gather(vg_words, v_words, 1)
+        for h in range(HALVES):
+            product(c_ps[:, cols(h)], g_codes, g_plane, vg_words, vg_plane, h)
+
+        th2 = sb.tile([P, PAGES], F32, name="th2")
+        alpha = sb.tile([P, PAGES], F32, name="alpha")
+        nc.scalar.activation(th2[:], th[:], ACT.Square)
+        nc.scalar.activation(pg[:, 7, :], th[:], ACT.Copy, scale=-0.25)
+        nc.scalar.activation(alpha[:], pg[:, 8, :], ACT.Square, scale=math.sqrt(PEN))
+        nc.scalar.activation(pg[:, 5, :], th2[:], ACT.Identity, scale=hc[:, 2:3], bias=hc[:, 3:4])
+        nc.scalar.activation(pg[:, 6, :], pg[:, 5, :], ACT.Square, scale=math.sqrt(PEN))
+
+        p = wide("p")
+        z = sb.tile([P, 1], F32, name="z")
+        nc.scalar.activation(p[:], s[:], ACT.Exp, bias=neg_max[:], accum_out=z[:])
+        nc.vector.scalar_tensor_tensor(pg[:, 4, :], pg[:, 5, :], PEN, pg[:, 8, :], ALU.mult, ALU.mult)
+        rz = sb.tile([P, 1], F32, name="rz")
+        nc.vector.reciprocal(rz[:], z[:])
+        pn = wide("pn")
+        nc.scalar.activation(pn[:], p[:], ACT.Copy, scale=rz[:])
+        cp = wide("cp")
+        c_mean = sb.tile([P, 1], F32, name="c_mean")
+        nc.vector.scalar_tensor_tensor(cp[:], c_ps[:], rz[:], p[:], ALU.mult, ALU.mult, accum_out=c_mean[:])
+        w = wide("w")
+        wa = wide("wa")
+        a_dot = sb.tile([P, PAGES], F32, name="a_dot")
+        for h in range(HALVES):
+            nc.vector.scalar_tensor_tensor(w[:, cols(h)], c_ps[:, cols(h)], c_mean[:], pn[:, cols(h)], ALU.subtract, ALU.mult)
+        w_sq = wide("w_sq")
+        nc.scalar.activation(w_sq[:], w[:], ACT.Square)
+        for h in range(HALVES):
+            nc.vector.tensor_tensor(wa[:, cols(h)], a_ps[h][:], w[:, cols(h)], ALU.mult)
+        for h in range(HALVES):
+            nc.vector.tensor_reduce(a_dot[:, pages(h)], by_page(wa[:, cols(h)]), AX.X, ALU.add)
+        nc.vector.tensor_reduce(nn[:, 1, 0:HP], by_page(w[:, cols(0)]), AX.X, ALU.add)
+        nc.vector.tensor_tensor(pg[:, 0:4, :], pg[:, 4:8, :], a_dot[:].unsqueeze(1).to_broadcast([P, 4, PAGES]), ALU.mult)
+        nc.vector.tensor_reduce(nn[:, 1, HP:PAGES], by_page(w[:, cols(1)]), AX.X, ALU.add)
+        c1b = sb.tile([P, PAGES], F32, name="c1b")
+        nc.vector.tensor_reduce(nn[:, 3, 0:HP], by_page(w_sq[:, cols(0)]), AX.X, ALU.add)
+        nc.vector.tensor_tensor(c1b[:], pg[:, 4, :], nn[:, 1, :], ALU.mult)
+        nc.vector.tensor_reduce(nn[:, 3, HP:PAGES], by_page(w_sq[:, cols(1)]), AX.X, ALU.add)
+        nc.vector.scalar_tensor_tensor(nn[:, 2, :], pg[:, 2, :], 16.0, c1b[:], ALU.mult, ALU.add)
+
+        f1 = wide("f1")
+        for g in range(PAGES):
+            sl = slice(g * PAGE, (g + 1) * PAGE)
+            nc.scalar.activation(f1[:, sl], w[:, sl], ACT.Identity, scale=alpha[:, g : g + 1], bias=pg[:, 0, g : g + 1])
+
+        ga = wide("ga")
+        f = wide("f")
+        for h in range(HALVES):
+            nc.vector.tensor_tensor(by_page(ga[:, cols(h)]), by_page(a_ps[h][:]), spread(nn[:, 2, pages(h)]), ALU.mult)
+        for h in range(HALVES):
+            nc.vector.tensor_tensor(f[:, cols(h)], f1[:, cols(h)], ga[:, cols(h)], ALU.add)
+        terms = sb.tile([P, 3, PAGES], F32, name="terms")
+        nc.vector.tensor_tensor(terms[:], pg[:, 2:5, :], nn[:, 1:4, :], ALU.mult)
+        fw = wide("fw")
+        fp = wide("fp")
+        h1 = sb.tile([P, 1], F32, name="h1")
+        neg_h0 = sb.tile([P, 1], F32, name="neg_h0")
+        nc.vector.scalar_tensor_tensor(fw[:], f[:], 1.0, w[:], ALU.mult, ALU.mult, accum_out=h1[:])
+        nc.vector.tensor_reduce(nn[:, 0, :], terms[:].rearrange("p r g -> p g r"), AX.X, ALU.add)
+        nc.vector.scalar_tensor_tensor(fp[:], f[:], -1.0, pn[:], ALU.mult, ALU.mult, accum_out=neg_h0[:])
+        neg_hs = wide("neg_hs")
+        last = sb.tile([P, 2, PAGES], F32, name="last")
+        nc.vector.scalar_tensor_tensor(neg_hs[:, cols(0)], pn[:, cols(0)], h1[:], fw[:, cols(0)], ALU.mult, ALU.subtract)
+        nc.vector.scalar_tensor_tensor(last[:], pg[:, 1:9:7, :], neg_h0[:], nn[:, 0:3:2, :], ALU.mult, ALU.add)
+        nc.vector.scalar_tensor_tensor(neg_hs[:, cols(1)], pn[:, cols(1)], h1[:], fw[:, cols(1)], ALU.mult, ALU.subtract)
+        y = wide("y")
+        for g in range(PAGES):
+            sl = slice(g * PAGE, (g + 1) * PAGE)
+            nc.scalar.activation(y[:, sl], w[:, sl], ACT.Identity, scale=last[:, 1, g : g + 1], bias=last[:, 0, g : g + 1])
+        hsa = wide("hsa")
+        neg_s = sb.tile([P, PAGES], F32, name="neg_s")
+        x = sb.tile([P, PAGES], F32, name="x")
+        for h in range(HALVES):
+            nc.vector.tensor_tensor(hsa[:, cols(h)], a_ps[h][:], neg_hs[:, cols(h)], ALU.mult)
+        for h in range(HALVES):
+            nc.vector.tensor_reduce(neg_s[:, pages(h)], by_page(hsa[:, cols(h)]), AX.X, ALU.add)
+        uh = wide("uh")
+        z0 = wide("z0")
+        z1 = wide("z1")
+        res = wide("res")
+        for h in range(HALVES):
+            nc.vector.tensor_tensor(by_page(uh[:, cols(h)]), by_page(neg_hs[:, cols(h)]), spread(pg[:, 8, pages(h)]), ALU.mult)
+        nc.vector.tensor_tensor(x[:], neg_s[:], pg[:, 5, :], ALU.mult)
+        for h in range(HALVES):
+            nc.vector.tensor_tensor(z0[:, cols(h)], base_sb[:, cols(h)], uh[:, cols(h)], ALU.subtract)
+        for h in range(HALVES):
+            nc.vector.tensor_tensor(z1[:, cols(h)], z0[:, cols(h)], y[:, cols(h)], ALU.add)
+        for h in range(HALVES):
+            nc.vector.tensor_tensor(by_page(res[:, cols(h)]), by_page(z1[:, cols(h)]), spread(x[:, pages(h)]), ALU.subtract)
+            nc.sync.dma_start(out=out[:, cols(h)], in_=res[:, cols(h)])

@@ -53,38 +53,35 @@ def tile_attend_gppagemates_kernel(tc, query, keys_words, keys_scales, helpf, go
 
         offsets = sb.tile([P, SLOTS // 16], U16, name="offsets")
         k_words = sb.tile([P, T], U16, name="k_words", align_bytes=64)
-        v_words = sb.tile([P, T], U16, name="v_words", align_bytes=64)
         k_plane = sb.tile([P, T], U8, name="k_plane", align_bytes=64)
-        v_plane = sb.tile([P, T], U8, name="v_plane", align_bytes=64)
-        q_raw = sb.tile([P, PACK, Q], F32, name="q_raw", align_bytes=64)
-        g_raw = sb.tile([P, PACK, Q], F32, name="g_raw", align_bytes=64)
+        v_plane = sb.tile([P, T], U8, name="v_plane", tag="v_plane", align_bytes=64)
+        q_raw = sb.tile([P, PACK, Q], F32, name="q_raw", tag="q_raw", align_bytes=64)
         help_col = sb.tile([P, 1], F32, name="help_col")
-        base_sb = wide("base_sb")
 
         nc.vector.memset(k_plane[:].bitcast(I32), 0)
-        nc.vector.memset(v_plane[:].bitcast(I32), 0)
-        warm = sb.tile([P, 2], F32, name="warm")
-        nc.gpsimd.memset(warm[:, 0:1], 0.0)
-        warm2 = sb.tile([P, 2], F32, name="warm2")
+        nc.gpsimd.memset(v_plane[:].bitcast(I32), 0)
+        warm = sb.tile([P, 2], F32, name="warm", tag="g_raw", align_bytes=64)
+        nc.vector.memset(warm[:, 0:1], 0.0)
+        warm2 = sb.tile([P, 2], F32, name="warm2", tag="v_words", align_bytes=64)
         nc.scalar.activation(warm2[:, 0:1], warm[:, 0:1], ACT.Exp)
 
+        nc.sync.dma_start(out=k_words[:].bitcast(I32), in_=keys_words[0].bitcast(I32))
         nc.sync.dma_start(offsets[:], offs)
-        for h in range(HALVES):
-            nc.sync.dma_start(out=k_words[:].bitcast(I32)[:, h * 512 : (h + 1) * 512], in_=keys_words[0].bitcast(I32)[:, h * 512 : (h + 1) * 512])
+        nc.gpsimd.dma_start(out=help_col[:], in_=helpf)
         nc.sync.dma_start(out=q_raw[:], in_=query.rearrange("(p j) w -> p j w", j=PACK))
-        nc.sync.dma_start(out=help_col[:], in_=helpf)
         load_scales(k_plane, keys_scales)
-        nc.sync.dma_start(out=g_raw[:], in_=gout.rearrange("(p j) w -> p j w", j=PACK))
         load_scales(v_plane, vals_scales)
+        g_raw = sb.tile([P, PACK, Q], F32, name="g_raw", tag="g_raw", align_bytes=64)
+        v_words = sb.tile([P, T], U16, name="v_words", tag="v_words", align_bytes=64)
+        nc.sync.dma_start(out=g_raw[:], in_=gout.rearrange("(p j) w -> p j w", j=PACK))
         nc.sync.dma_start(out=v_words[:].bitcast(I32), in_=vals_words[0].bitcast(I32))
-        nc.sync.dma_start(out=base_sb[:], in_=base)
 
         hc = sb.tile([P, 4], F32, name="hc")
         for j, (mul, add) in enumerate(((0.5, 0.0), (0.5, 1.0), (-1.0 / 16, 0.0), (1.0 / 16, 0.0))):
             nc.gpsimd.tensor_scalar(hc[:, j : j + 1], help_col[:], mul, add, ALU.mult, ALU.add)
 
         def cast(raw, name):
-            grouped = sb.tile([P, Q, PACK], BF16, name=name + "_bf", align_bytes=64)
+            grouped = sb.tile([P, Q, PACK], BF16, name=name + "_bf", tag=name + "_bf", align_bytes=64)
             nc.scalar.copy(grouped[:], raw[:].rearrange("p j w -> p w j"))
             return grouped
 
@@ -94,70 +91,73 @@ def tile_attend_gppagemates_kernel(tc, query, keys_words, keys_scales, helpf, go
             nc.vector.quantize_mx(out=codes[:].bitcast(FP8X4), scales=plane[:], in_=grouped[:].rearrange("p w j -> p (w j)"))
             return codes, plane
 
-        def gather(dst, window, h):
-            nc.vector.tensor_copy(dst[:, cols(h)], window[:].indirect(offsets[:, pages(h)]))
+        def gather(dst, window, listed):
+            nc.vector.tensor_copy(dst, window[:].indirect(listed))
 
-        def product(dst, codes, plane, words, wplane, h):
-            nc.tensor.matmul_mx(out=dst, lhsT=codes[:].bitcast(FP8X4), lhsT_scale=plane[:], rhs=words[:, cols(h)].bitcast(FP4X4), rhs_scale=wplane[:, cols(h)], start=True, stop=True)
+        def product(dst, codes, plane, words, wplane):
+            nc.tensor.matmul_mx(out=dst, lhsT=codes[:].bitcast(FP8X4), lhsT_scale=plane[:], rhs=words.bitcast(FP4X4), rhs_scale=wplane, start=True, stop=True)
 
         kg_words = sb.tile([P, SLOTS], U16, name="kg_words", align_bytes=64)
         kg_plane = sb.tile([P, SLOTS], U8, name="kg_plane", align_bytes=64)
-        vg_words = sb.tile([P, SLOTS], U16, name="vg_words", align_bytes=64)
         vg_plane = sb.tile([P, SLOTS], U8, name="vg_plane", align_bytes=64)
         a_ps = [ps.tile([P, HS], F32, name="a_ps%d" % h) for h in range(HALVES)]
         c_ps = ps.tile([P, SLOTS], F32, name="c_ps")
 
         q_bf = cast(q_raw, "q")
-        gather(kg_words, k_words, 0)
-        gather(kg_words, k_words, 1)
-        gather(kg_plane, k_plane, 0)
+        g_bf = cast(g_raw, "g")
+        gather(kg_words[:], k_words, offsets[:])
+        gather(kg_plane[:], k_plane, offsets[:])
         q_codes, q_plane = quantise(q_bf, "q")
-        gather(kg_plane, k_plane, 1)
+        base_sb = sb.tile([P, SLOTS], F32, name="base_sb", tag="q_bf", align_bytes=64)
+        nc.sync.dma_start(out=base_sb[:], in_=base)
         for h in range(HALVES):
-            product(a_ps[h][:], q_codes, q_plane, kg_words, kg_plane, h)
+            product(a_ps[h][:], q_codes, q_plane, kg_words[:, cols(h)], kg_plane[:, cols(h)])
 
-        pg = sb.tile([P, 9, PAGES], F32, name="pg")
+        gather(vg_plane[:], v_plane, offsets[:])
+        pg = sb.tile([P, 8, PAGES], F32, name="pg")
         nn = sb.tile([P, 4, PAGES], F32, name="nn")
-        a_sum = sb.tile([P, PAGES], F32, name="a_sum")
-        th = sb.tile([P, PAGES], F32, name="th")
-        s = wide("s")
+        a_sum = sb.tile([P, PAGES], F32, name="a_sum", tag="v_plane", align_bytes=64)
+        th = sb.tile([P, PAGES], F32, name="th", tag="g_raw", align_bytes=64)
         for h in range(HALVES):
             nc.vector.tensor_reduce(a_sum[:, pages(h)], by_page(a_ps[h][:]), AX.X, ALU.add)
         for h in range(HALVES):
             nc.scalar.activation(th[:, pages(h)], a_sum[:, pages(h)], ACT.Tanh, scale=2.0 / PAGE)
-            nc.scalar.activation(pg[:, 8, pages(h)], th[:, pages(h)], ACT.Identity, scale=hc[:, 0:1], bias=hc[:, 1:2])
-        g_bf = cast(g_raw, "g")
-        gather(vg_plane, v_plane, 0)
-        gather(vg_plane, v_plane, 1)
-        for h in range(HALVES):
-            nc.vector.tensor_tensor(by_page(s[:, cols(h)]), by_page(a_ps[h][:]), spread(pg[:, 8, pages(h)]), ALU.mult)
+            nc.scalar.activation(pg[:, 7, pages(h)], th[:, pages(h)], ACT.Identity, scale=hc[:, 0:1], bias=hc[:, 1:2])
         g_codes, g_plane = quantise(g_bf, "g")
-        gather(vg_words, v_words, 0)
-        neg_max = sb.tile([P, 1], F32, name="neg_max")
-        nc.vector.tensor_reduce(neg_max[:], s[:], AX.X, ALU.max, negate=True)
-        gather(vg_words, v_words, 1)
+        vg_words0 = sb.tile([P, HS], U16, name="vg_words0", align_bytes=64)
+        gather(vg_words0[:], v_words, offsets[:, pages(0)])
+        s = wide("s")
         for h in range(HALVES):
-            product(c_ps[:, cols(h)], g_codes, g_plane, vg_words, vg_plane, h)
-
-        th2 = sb.tile([P, PAGES], F32, name="th2")
-        alpha = sb.tile([P, PAGES], F32, name="alpha")
-        nc.scalar.activation(th2[:], th[:], ACT.Square)
-        nc.scalar.activation(pg[:, 7, :], th[:], ACT.Copy, scale=-0.25)
-        nc.scalar.activation(alpha[:], pg[:, 8, :], ACT.Square, scale=math.sqrt(PEN))
-        nc.scalar.activation(pg[:, 5, :], th2[:], ACT.Identity, scale=hc[:, 2:3], bias=hc[:, 3:4])
-        nc.scalar.activation(pg[:, 6, :], pg[:, 5, :], ACT.Square, scale=math.sqrt(PEN))
+            nc.vector.tensor_tensor(by_page(s[:, cols(h)]), by_page(a_ps[h][:]), spread(pg[:, 7, pages(h)]), ALU.mult)
+        half_max = [sb.tile([P, 1], F32, name="half_max%d" % h, tag="half_max%d" % h, align_bytes=64) for h in range(HALVES)]
+        for h in range(HALVES):
+            nc.vector.tensor_reduce(half_max[h][:], s[:, cols(h)], AX.X, ALU.max, negate=True)
+        neg_max = sb.tile([P, 1], F32, name="neg_max")
+        nc.vector.tensor_tensor(neg_max[:], half_max[0][:], half_max[1][:], ALU.min)
+        vg_words1 = sb.tile([P, HS], U16, name="vg_words1", tag="half_max0", align_bytes=64)
+        gather(vg_words1[:], v_words, offsets[:, pages(1)])
+        for h, words in enumerate((vg_words0, vg_words1)):
+            product(c_ps[:, cols(h)], g_codes, g_plane, words[:], vg_plane[:, cols(h)])
 
         p = wide("p")
         z = sb.tile([P, 1], F32, name="z")
         nc.scalar.activation(p[:], s[:], ACT.Exp, bias=neg_max[:], accum_out=z[:])
-        nc.vector.scalar_tensor_tensor(pg[:, 4, :], pg[:, 5, :], PEN, pg[:, 8, :], ALU.mult, ALU.mult)
-        rz = sb.tile([P, 1], F32, name="rz")
+        th2 = sb.tile([P, PAGES], F32, name="th2")
+        alpha = sb.tile([P, PAGES], F32, name="alpha")
+        nc.scalar.activation(th2[:], th[:], ACT.Square)
+        nc.scalar.activation(pg[:, 5, :], th[:], ACT.Copy, scale=-0.25)
+        nc.scalar.activation(alpha[:], pg[:, 7, :], ACT.Square, scale=math.sqrt(PEN))
+        nc.scalar.activation(pg[:, 6, :], th2[:], ACT.Identity, scale=hc[:, 2:3], bias=hc[:, 3:4])
+        nc.scalar.activation(pg[:, 4, :], pg[:, 6, :], ACT.Square, scale=math.sqrt(PEN))
+
+        rz = sb.tile([P, 1], F32, name="rz", tag="v_words", align_bytes=64)
         nc.vector.reciprocal(rz[:], z[:])
         pn = wide("pn")
         nc.scalar.activation(pn[:], p[:], ACT.Copy, scale=rz[:])
         cp = wide("cp")
         c_mean = sb.tile([P, 1], F32, name="c_mean")
         nc.vector.scalar_tensor_tensor(cp[:], c_ps[:], rz[:], p[:], ALU.mult, ALU.mult, accum_out=c_mean[:])
+        nc.vector.scalar_tensor_tensor(pg[:, 3, :], pg[:, 6, :], PEN, pg[:, 7, :], ALU.mult, ALU.mult)
         w = wide("w")
         wa = wide("wa")
         a_dot = sb.tile([P, PAGES], F32, name="a_dot")
@@ -170,13 +170,13 @@ def tile_attend_gppagemates_kernel(tc, query, keys_words, keys_scales, helpf, go
         for h in range(HALVES):
             nc.vector.tensor_reduce(a_dot[:, pages(h)], by_page(wa[:, cols(h)]), AX.X, ALU.add)
         nc.vector.tensor_reduce(nn[:, 1, 0:HP], by_page(w[:, cols(0)]), AX.X, ALU.add)
-        nc.vector.tensor_tensor(pg[:, 0:4, :], pg[:, 4:8, :], a_dot[:].unsqueeze(1).to_broadcast([P, 4, PAGES]), ALU.mult)
+        nc.vector.tensor_tensor(pg[:, 0:3, :], pg[:, 3:6, :], a_dot[:].unsqueeze(1).to_broadcast([P, 3, PAGES]), ALU.mult)
         nc.vector.tensor_reduce(nn[:, 1, HP:PAGES], by_page(w[:, cols(1)]), AX.X, ALU.add)
         c1b = sb.tile([P, PAGES], F32, name="c1b")
         nc.vector.tensor_reduce(nn[:, 3, 0:HP], by_page(w_sq[:, cols(0)]), AX.X, ALU.add)
-        nc.vector.tensor_tensor(c1b[:], pg[:, 4, :], nn[:, 1, :], ALU.mult)
+        nc.vector.tensor_tensor(c1b[:], pg[:, 3, :], nn[:, 1, :], ALU.mult)
         nc.vector.tensor_reduce(nn[:, 3, HP:PAGES], by_page(w_sq[:, cols(1)]), AX.X, ALU.add)
-        nc.vector.scalar_tensor_tensor(nn[:, 2, :], pg[:, 2, :], 16.0, c1b[:], ALU.mult, ALU.add)
+        nc.vector.scalar_tensor_tensor(nn[:, 2, :], pg[:, 1, :], 16.0, c1b[:], ALU.mult, ALU.add)
 
         f1 = wide("f1")
         for g in range(PAGES):
@@ -185,28 +185,33 @@ def tile_attend_gppagemates_kernel(tc, query, keys_words, keys_scales, helpf, go
 
         ga = wide("ga")
         f = wide("f")
-        for h in range(HALVES):
-            nc.vector.tensor_tensor(by_page(ga[:, cols(h)]), by_page(a_ps[h][:]), spread(nn[:, 2, pages(h)]), ALU.mult)
+        terms = sb.tile([P, 3, PAGES], F32, name="terms")
+        nc.vector.tensor_tensor(by_page(ga[:, cols(0)]), by_page(a_ps[0][:]), spread(nn[:, 2, pages(0)]), ALU.mult)
+        nc.vector.tensor_tensor(terms[:], pg[:, 1:4, :], nn[:, 1:4, :], ALU.mult)
+        nc.vector.tensor_tensor(by_page(ga[:, cols(1)]), by_page(a_ps[1][:]), spread(nn[:, 2, pages(1)]), ALU.mult)
+        nc.vector.tensor_reduce(nn[:, 0, :], terms[:].rearrange("p r g -> p g r"), AX.X, ALU.add)
         for h in range(HALVES):
             nc.vector.tensor_tensor(f[:, cols(h)], f1[:, cols(h)], ga[:, cols(h)], ALU.add)
-        terms = sb.tile([P, 3, PAGES], F32, name="terms")
-        nc.vector.tensor_tensor(terms[:], pg[:, 2:5, :], nn[:, 1:4, :], ALU.mult)
         fw = wide("fw")
         fp = wide("fp")
         h1 = sb.tile([P, 1], F32, name="h1")
         neg_h0 = sb.tile([P, 1], F32, name="neg_h0")
-        nc.vector.scalar_tensor_tensor(fw[:], f[:], 1.0, w[:], ALU.mult, ALU.mult, accum_out=h1[:])
-        nc.vector.tensor_reduce(nn[:, 0, :], terms[:].rearrange("p r g -> p g r"), AX.X, ALU.add)
-        nc.vector.scalar_tensor_tensor(fp[:], f[:], -1.0, pn[:], ALU.mult, ALU.mult, accum_out=neg_h0[:])
-        neg_hs = wide("neg_hs")
-        last = sb.tile([P, 2, PAGES], F32, name="last")
-        nc.vector.scalar_tensor_tensor(neg_hs[:, cols(0)], pn[:, cols(0)], h1[:], fw[:, cols(0)], ALU.mult, ALU.subtract)
-        nc.vector.scalar_tensor_tensor(last[:], pg[:, 1:9:7, :], neg_h0[:], nn[:, 0:3:2, :], ALU.mult, ALU.add)
-        nc.vector.scalar_tensor_tensor(neg_hs[:, cols(1)], pn[:, cols(1)], h1[:], fw[:, cols(1)], ALU.mult, ALU.subtract)
         y = wide("y")
         for g in range(PAGES):
             sl = slice(g * PAGE, (g + 1) * PAGE)
-            nc.scalar.activation(y[:, sl], w[:, sl], ACT.Identity, scale=last[:, 1, g : g + 1], bias=last[:, 0, g : g + 1])
+            nc.scalar.activation(y[:, sl], w[:, sl], ACT.Identity, scale=nn[:, 2, g : g + 1], bias=nn[:, 0, g : g + 1])
+        z0 = wide("z0")
+        nc.vector.scalar_tensor_tensor(fp[:], f[:], -1.0, pn[:], ALU.mult, ALU.mult, accum_out=neg_h0[:])
+        nc.vector.tensor_tensor(z0[:, cols(0)], base_sb[:, cols(0)], y[:, cols(0)], ALU.add)
+        nc.vector.scalar_tensor_tensor(fw[:], f[:], neg_h0[:], w[:], ALU.add, ALU.mult, accum_out=h1[:])
+        nc.vector.tensor_tensor(z0[:, cols(1)], base_sb[:, cols(1)], y[:, cols(1)], ALU.add)
+        neg_hs = wide("neg_hs")
+        for h in range(HALVES):
+            nc.vector.scalar_tensor_tensor(neg_hs[:, cols(h)], pn[:, cols(h)], h1[:], fw[:, cols(h)], ALU.mult, ALU.subtract)
+        uh = wide("uh")
+        for g in range(PAGES):
+            sl = slice(g * PAGE, (g + 1) * PAGE)
+            nc.scalar.activation(uh[:, sl], neg_hs[:, sl], ACT.Copy, scale=pg[:, 7, g : g + 1])
         hsa = wide("hsa")
         neg_s = sb.tile([P, PAGES], F32, name="neg_s")
         x = sb.tile([P, PAGES], F32, name="x")
@@ -214,17 +219,11 @@ def tile_attend_gppagemates_kernel(tc, query, keys_words, keys_scales, helpf, go
             nc.vector.tensor_tensor(hsa[:, cols(h)], a_ps[h][:], neg_hs[:, cols(h)], ALU.mult)
         for h in range(HALVES):
             nc.vector.tensor_reduce(neg_s[:, pages(h)], by_page(hsa[:, cols(h)]), AX.X, ALU.add)
-        uh = wide("uh")
-        z0 = wide("z0")
         z1 = wide("z1")
         res = wide("res")
-        for h in range(HALVES):
-            nc.vector.tensor_tensor(by_page(uh[:, cols(h)]), by_page(neg_hs[:, cols(h)]), spread(pg[:, 8, pages(h)]), ALU.mult)
-        nc.vector.tensor_tensor(x[:], neg_s[:], pg[:, 5, :], ALU.mult)
-        for h in range(HALVES):
-            nc.vector.tensor_tensor(z0[:, cols(h)], base_sb[:, cols(h)], uh[:, cols(h)], ALU.subtract)
-        for h in range(HALVES):
-            nc.vector.tensor_tensor(z1[:, cols(h)], z0[:, cols(h)], y[:, cols(h)], ALU.add)
+        nc.vector.tensor_tensor(z1[:, cols(0)], z0[:, cols(0)], uh[:, cols(0)], ALU.subtract)
+        nc.vector.tensor_tensor(x[:], neg_s[:], pg[:, 6, :], ALU.mult)
+        nc.vector.tensor_tensor(z1[:, cols(1)], z0[:, cols(1)], uh[:, cols(1)], ALU.subtract)
         for h in range(HALVES):
             nc.vector.tensor_tensor(by_page(res[:, cols(h)]), by_page(z1[:, cols(h)]), spread(x[:, pages(h)]), ALU.subtract)
-            nc.sync.dma_start(out=out[:, cols(h)], in_=res[:, cols(h)])
+            (nc.sync, nc.scalar)[h].dma_start(out=out[:, cols(h)], in_=res[:, cols(h)])

@@ -48,8 +48,8 @@ def tile_attend_gppagemates_kernel(tc, query, keys_words, keys_scales, helpf, go
             return ap.unsqueeze(2).to_broadcast([P, ap.shape[1], PAGE])
 
         def load_scales(plane, scales):
-            for quad in range(4):
-                nc.sync.dma_start(out=plane[32 * quad : 32 * quad + 4, :].bitcast(I32), in_=scales[0, 4 * quad : 4 * quad + 4, :].bitcast(I32))
+            for r in range(4):
+                nc.sync.dma_start(out=plane[:].bitcast(I32)[r:P:32, :], in_=scales[0].bitcast(I32)[r:16:4, :])
 
         offsets = sb.tile([P, SLOTS // 16], U16, name="offsets")
         k_words = sb.tile([P, T], U16, name="k_words", align_bytes=64)
@@ -59,15 +59,15 @@ def tile_attend_gppagemates_kernel(tc, query, keys_words, keys_scales, helpf, go
         help_col = sb.tile([P, 1], F32, name="help_col")
 
         nc.vector.memset(k_plane[:].bitcast(I32), 0)
-        nc.gpsimd.memset(v_plane[:].bitcast(I32), 0)
         warm = sb.tile([P, 2], F32, name="warm", tag="g_raw", align_bytes=64)
         nc.vector.memset(warm[:, 0:1], 0.0)
+        nc.vector.memset(v_plane[:].bitcast(I32), 0)
         warm2 = sb.tile([P, 2], F32, name="warm2", tag="v_words", align_bytes=64)
         nc.scalar.activation(warm2[:, 0:1], warm[:, 0:1], ACT.Exp)
 
         nc.sync.dma_start(out=k_words[:].bitcast(I32), in_=keys_words[0].bitcast(I32))
         nc.sync.dma_start(offsets[:], offs)
-        nc.gpsimd.dma_start(out=help_col[:], in_=helpf)
+        nc.sync.dma_start(out=help_col[:], in_=helpf)
         nc.sync.dma_start(out=q_raw[:], in_=query.rearrange("(p j) w -> p j w", j=PACK))
         load_scales(k_plane, keys_scales)
         load_scales(v_plane, vals_scales)
@@ -78,7 +78,7 @@ def tile_attend_gppagemates_kernel(tc, query, keys_words, keys_scales, helpf, go
 
         hc = sb.tile([P, 4], F32, name="hc")
         for j, (mul, add) in enumerate(((0.5, 0.0), (0.5, 1.0), (-1.0 / 16, 0.0), (1.0 / 16, 0.0))):
-            nc.gpsimd.tensor_scalar(hc[:, j : j + 1], help_col[:], mul, add, ALU.mult, ALU.add)
+            nc.scalar.activation(hc[:, j : j + 1], help_col[:], ACT.Copy, scale=mul, bias=add)
 
         def cast(raw, name):
             grouped = sb.tile([P, Q, PACK], BF16, name=name + "_bf", tag=name + "_bf", align_bytes=64)
@@ -226,4 +226,4 @@ def tile_attend_gppagemates_kernel(tc, query, keys_words, keys_scales, helpf, go
         nc.vector.tensor_tensor(z1[:, cols(1)], z0[:, cols(1)], uh[:, cols(1)], ALU.subtract)
         for h in range(HALVES):
             nc.vector.tensor_tensor(by_page(res[:, cols(h)]), by_page(z1[:, cols(h)]), spread(x[:, pages(h)]), ALU.subtract)
-            (nc.sync, nc.scalar)[h].dma_start(out=out[:, cols(h)], in_=res[:, cols(h)])
+            nc.sync.dma_start(out=out[:, cols(h)], in_=res[:, cols(h)])

@@ -3,15 +3,19 @@ from contextlib import ExitStack
 
 import concourse.mybir as mybir
 
-D, T, SLOTS, Q = 512, 2048, 512, 128
+DEPTH, TOKENS, SLOTS, ROWS = 512, 2048, 512, 128
 PAGES, PAGE = 32, 16
-FLOPS = 2 * 2 * D * Q * SLOTS
+FLOPS = 2 * 2 * DEPTH * ROWS * SLOTS
 P = 128
 PACK = 4
+SCALE_ROWS = DEPTH // 32
 HALVES = 2
-HS = SLOTS // HALVES
-HP = PAGES // HALVES
-PEN = 512.0 * 2.0 * 512.0
+HALF_SLOTS = SLOTS // HALVES
+HALF_PAGES = PAGES // HALVES
+K = 512.0 * 2.0 * 512.0
+
+BETA, C3A, TA, C1, C3, TQ, HV, U = range(8)
+REST, B, GAMMA, W = range(4)
 
 F32 = mybir.dt.float32
 BF16 = mybir.dt.bfloat16
@@ -26,6 +30,26 @@ ACT = mybir.ActivationFunctionType
 AX = mybir.AxisListType
 
 
+def cols(half):
+    return slice(half * HALF_SLOTS, (half + 1) * HALF_SLOTS)
+
+
+def pages(half):
+    return slice(half * HALF_PAGES, (half + 1) * HALF_PAGES)
+
+
+def page_cols(page):
+    return slice(page * PAGE, (page + 1) * PAGE)
+
+
+def by_page(ap):
+    return ap.rearrange("p (g j) -> p g j", j=PAGE)
+
+
+def spread(ap):
+    return ap.unsqueeze(2).to_broadcast([P, ap.shape[1], PAGE])
+
+
 def tile_attend_gppagemates_kernel(tc, query, keys_words, keys_scales, helpf, gout, vals_words, vals_scales, base, offs, out):
     nc = tc.nc
     with ExitStack() as ctx:
@@ -35,72 +59,58 @@ def tile_attend_gppagemates_kernel(tc, query, keys_words, keys_scales, helpf, go
         def wide(name):
             return sb.tile([P, SLOTS], F32, name=name, align_bytes=64)
 
-        def cols(h):
-            return slice(h * HS, (h + 1) * HS)
-
-        def pages(h):
-            return slice(h * HP, (h + 1) * HP)
-
-        def by_page(ap):
-            return ap.rearrange("p (g j) -> p g j", j=PAGE)
-
-        def spread(ap):
-            return ap.unsqueeze(2).to_broadcast([P, ap.shape[1], PAGE])
-
         def load_scales(plane, scales):
             for r in range(4):
-                nc.sync.dma_start(out=plane[:].bitcast(I32)[r:P:32, :], in_=scales[0].bitcast(I32)[r:16:4, :])
-
-        offsets = sb.tile([P, SLOTS // 16], U16, name="offsets")
-        k_words = sb.tile([P, T], U16, name="k_words", align_bytes=64)
-        k_plane = sb.tile([P, T], U8, name="k_plane", align_bytes=64)
-        v_plane = sb.tile([P, T], U8, name="v_plane", tag="v_plane", align_bytes=64)
-        q_raw = sb.tile([P, PACK, Q], F32, name="q_raw", tag="q_raw", align_bytes=64)
-        help_col = sb.tile([P, 1], F32, name="help_col")
-
-        nc.vector.memset(k_plane[:].bitcast(I32), 0)
-        warm = sb.tile([P, 2], F32, name="warm", tag="g_raw", align_bytes=64)
-        nc.vector.memset(warm[:, 0:1], 0.0)
-        nc.vector.memset(v_plane[:].bitcast(I32), 0)
-        warm2 = sb.tile([P, 2], F32, name="warm2", tag="v_words", align_bytes=64)
-        nc.scalar.activation(warm2[:, 0:1], warm[:, 0:1], ACT.Exp)
-
-        nc.sync.dma_start(out=k_words[:].bitcast(I32), in_=keys_words[0].bitcast(I32))
-        nc.sync.dma_start(offsets[:], offs)
-        nc.sync.dma_start(out=help_col[:], in_=helpf)
-        nc.sync.dma_start(out=q_raw[:], in_=query.rearrange("(p j) w -> p j w", j=PACK))
-        load_scales(k_plane, keys_scales)
-        load_scales(v_plane, vals_scales)
-        g_raw = sb.tile([P, PACK, Q], F32, name="g_raw", tag="g_raw", align_bytes=64)
-        v_words = sb.tile([P, T], U16, name="v_words", tag="v_words", align_bytes=64)
-        nc.sync.dma_start(out=g_raw[:], in_=gout.rearrange("(p j) w -> p j w", j=PACK))
-        nc.sync.dma_start(out=v_words[:].bitcast(I32), in_=vals_words[0].bitcast(I32))
-
-        hc = sb.tile([P, 4], F32, name="hc")
-        for j, (mul, add) in enumerate(((0.5, 0.0), (0.5, 1.0), (-1.0 / 16, 0.0), (1.0 / 16, 0.0))):
-            nc.scalar.activation(hc[:, j : j + 1], help_col[:], ACT.Copy, scale=mul, bias=add)
+                nc.sync.dma_start(out=plane[:].bitcast(I32)[r:P:32, :], in_=scales[0].bitcast(I32)[r:SCALE_ROWS:4, :])
 
         def cast(raw, name):
-            grouped = sb.tile([P, Q, PACK], BF16, name=name + "_bf", tag=name + "_bf", align_bytes=64)
+            grouped = sb.tile([P, ROWS, PACK], BF16, name=name + "_bf", tag=name + "_bf", align_bytes=64)
             nc.scalar.copy(grouped[:], raw[:].rearrange("p j w -> p w j"))
             return grouped
 
         def quantise(grouped, name):
-            codes = sb.tile([P, Q], U32, name=name + "_codes", align_bytes=64)
-            plane = sb.tile([P, Q], U8, name=name + "_plane", align_bytes=64)
+            codes = sb.tile([P, ROWS], U32, name=name + "_codes", align_bytes=64)
+            plane = sb.tile([P, ROWS], U8, name=name + "_plane", align_bytes=64)
             nc.vector.quantize_mx(out=codes[:].bitcast(FP8X4), scales=plane[:], in_=grouped[:].rearrange("p w j -> p (w j)"))
             return codes, plane
 
         def gather(dst, window, listed):
             nc.vector.tensor_copy(dst, window[:].indirect(listed))
 
-        def product(dst, codes, plane, words, wplane):
-            nc.tensor.matmul_mx(out=dst, lhsT=codes[:].bitcast(FP8X4), lhsT_scale=plane[:], rhs=words.bitcast(FP4X4), rhs_scale=wplane, start=True, stop=True)
+        def product(dst, codes, plane, words, words_plane):
+            nc.tensor.matmul_mx(out=dst, lhsT=codes[:].bitcast(FP8X4), lhsT_scale=plane[:], rhs=words.bitcast(FP4X4), rhs_scale=words_plane, start=True, stop=True)
+
+        offsets = sb.tile([P, SLOTS // 16], U16, name="offsets")
+        k_words = sb.tile([P, TOKENS], U16, name="k_words", align_bytes=64)
+        k_plane = sb.tile([P, TOKENS], U8, name="k_plane", align_bytes=64)
+        v_plane = sb.tile([P, TOKENS], U8, name="v_plane", tag="v_plane", align_bytes=64)
+        q_raw = sb.tile([P, PACK, ROWS], F32, name="q_raw", tag="q_raw", align_bytes=64)
+        help_col = sb.tile([P, 1], F32, name="help_col")
+
+        nc.vector.memset(k_plane[:].bitcast(I32), 0)
+        nc.vector.memset(v_plane[:].bitcast(I32), 0)
+
+        nc.sync.dma_start(out=k_words[:].bitcast(I32), in_=keys_words[0].bitcast(I32))
+        nc.sync.dma_start(offsets[:], offs)
+        nc.sync.dma_start(out=help_col[:], in_=helpf)
+        load_scales(k_plane, keys_scales)
+        nc.sync.dma_start(out=q_raw[:], in_=query.rearrange("(p j) w -> p j w", j=PACK))
+        load_scales(v_plane, vals_scales)
+        g_raw = sb.tile([P, PACK, ROWS], F32, name="g_raw", tag="g_raw", align_bytes=64)
+        v_words = sb.tile([P, TOKENS], U16, name="v_words", tag="v_words", align_bytes=64)
+        nc.sync.dma_start(out=g_raw[:], in_=gout.rearrange("(p j) w -> p j w", j=PACK))
+        nc.sync.dma_start(out=v_words[:].bitcast(I32), in_=vals_words[0].bitcast(I32))
+        base_sb = wide("base_sb")
+        nc.sync.dma_start(out=base_sb[:], in_=base)
+
+        row_fac = sb.tile([P, 4], F32, name="row_fac")
+        for j, (times, plus) in enumerate(((0.5, 0.0), (0.5, 1.0), (-1.0 / 16, 0.0), (1.0 / 16, 0.0))):
+            nc.scalar.activation(row_fac[:, j : j + 1], help_col[:], ACT.Copy, scale=times, bias=plus)
 
         kg_words = sb.tile([P, SLOTS], U16, name="kg_words", align_bytes=64)
         kg_plane = sb.tile([P, SLOTS], U8, name="kg_plane", align_bytes=64)
         vg_plane = sb.tile([P, SLOTS], U8, name="vg_plane", align_bytes=64)
-        a_ps = [ps.tile([P, HS], F32, name="a_ps%d" % h) for h in range(HALVES)]
+        a_ps = [ps.tile([P, HALF_SLOTS], F32, name="a_ps%d" % h) for h in range(HALVES)]
         c_ps = ps.tile([P, SLOTS], F32, name="c_ps")
 
         q_bf = cast(q_raw, "q")
@@ -108,33 +118,32 @@ def tile_attend_gppagemates_kernel(tc, query, keys_words, keys_scales, helpf, go
         gather(kg_words[:], k_words, offsets[:])
         gather(kg_plane[:], k_plane, offsets[:])
         q_codes, q_plane = quantise(q_bf, "q")
-        base_sb = sb.tile([P, SLOTS], F32, name="base_sb", tag="q_bf", align_bytes=64)
-        nc.sync.dma_start(out=base_sb[:], in_=base)
         for h in range(HALVES):
             product(a_ps[h][:], q_codes, q_plane, kg_words[:, cols(h)], kg_plane[:, cols(h)])
 
         gather(vg_plane[:], v_plane, offsets[:])
-        pg = sb.tile([P, 8, PAGES], F32, name="pg")
-        nn = sb.tile([P, 4, PAGES], F32, name="nn")
+        coef = sb.tile([P, 8, PAGES], F32, name="coef")
+        sums = sb.tile([P, 4, PAGES], F32, name="sums")
         a_sum = sb.tile([P, PAGES], F32, name="a_sum", tag="v_plane", align_bytes=64)
         th = sb.tile([P, PAGES], F32, name="th", tag="g_raw", align_bytes=64)
         for h in range(HALVES):
             nc.vector.tensor_reduce(a_sum[:, pages(h)], by_page(a_ps[h][:]), AX.X, ALU.add)
         for h in range(HALVES):
             nc.scalar.activation(th[:, pages(h)], a_sum[:, pages(h)], ACT.Tanh, scale=2.0 / PAGE)
-            nc.scalar.activation(pg[:, 7, pages(h)], th[:, pages(h)], ACT.Identity, scale=hc[:, 0:1], bias=hc[:, 1:2])
+            nc.scalar.activation(coef[:, U, pages(h)], th[:, pages(h)], ACT.Identity, scale=row_fac[:, 0:1], bias=row_fac[:, 1:2])
         g_codes, g_plane = quantise(g_bf, "g")
-        vg_words0 = sb.tile([P, HS], U16, name="vg_words0", align_bytes=64)
+        vg_words0 = sb.tile([P, HALF_SLOTS], U16, name="vg_words0", align_bytes=64)
         gather(vg_words0[:], v_words, offsets[:, pages(0)])
+
         s = wide("s")
         for h in range(HALVES):
-            nc.vector.tensor_tensor(by_page(s[:, cols(h)]), by_page(a_ps[h][:]), spread(pg[:, 7, pages(h)]), ALU.mult)
+            nc.vector.tensor_tensor(by_page(s[:, cols(h)]), by_page(a_ps[h][:]), spread(coef[:, U, pages(h)]), ALU.mult)
         half_max = [sb.tile([P, 1], F32, name="half_max%d" % h, tag="half_max%d" % h, align_bytes=64) for h in range(HALVES)]
         for h in range(HALVES):
             nc.vector.tensor_reduce(half_max[h][:], s[:, cols(h)], AX.X, ALU.max, negate=True)
         neg_max = sb.tile([P, 1], F32, name="neg_max")
         nc.vector.tensor_tensor(neg_max[:], half_max[0][:], half_max[1][:], ALU.min)
-        vg_words1 = sb.tile([P, HS], U16, name="vg_words1", tag="half_max0", align_bytes=64)
+        vg_words1 = sb.tile([P, HALF_SLOTS], U16, name="vg_words1", tag="half_max0", align_bytes=64)
         gather(vg_words1[:], v_words, offsets[:, pages(1)])
         for h, words in enumerate((vg_words0, vg_words1)):
             product(c_ps[:, cols(h)], g_codes, g_plane, words[:], vg_plane[:, cols(h)])
@@ -142,88 +151,88 @@ def tile_attend_gppagemates_kernel(tc, query, keys_words, keys_scales, helpf, go
         p = wide("p")
         z = sb.tile([P, 1], F32, name="z")
         nc.scalar.activation(p[:], s[:], ACT.Exp, bias=neg_max[:], accum_out=z[:])
-        th2 = sb.tile([P, PAGES], F32, name="th2")
+        th_sq = sb.tile([P, PAGES], F32, name="th_sq")
         alpha = sb.tile([P, PAGES], F32, name="alpha")
-        nc.scalar.activation(th2[:], th[:], ACT.Square)
-        nc.scalar.activation(pg[:, 5, :], th[:], ACT.Copy, scale=-0.25)
-        nc.scalar.activation(alpha[:], pg[:, 7, :], ACT.Square, scale=math.sqrt(PEN))
-        nc.scalar.activation(pg[:, 6, :], th2[:], ACT.Identity, scale=hc[:, 2:3], bias=hc[:, 3:4])
-        nc.scalar.activation(pg[:, 4, :], pg[:, 6, :], ACT.Square, scale=math.sqrt(PEN))
+        nc.scalar.activation(th_sq[:], th[:], ACT.Square)
+        nc.scalar.activation(coef[:, TQ, :], th[:], ACT.Copy, scale=-0.25)
+        nc.scalar.activation(alpha[:], coef[:, U, :], ACT.Square, scale=math.sqrt(K))
+        nc.scalar.activation(coef[:, HV, :], th_sq[:], ACT.Identity, scale=row_fac[:, 2:3], bias=row_fac[:, 3:4])
+        nc.scalar.activation(coef[:, C3, :], coef[:, HV, :], ACT.Square, scale=math.sqrt(K))
 
         rz = sb.tile([P, 1], F32, name="rz", tag="v_words", align_bytes=64)
         nc.vector.reciprocal(rz[:], z[:])
-        pn = wide("pn")
-        nc.scalar.activation(pn[:], p[:], ACT.Copy, scale=rz[:])
-        cp = wide("cp")
+        prob = wide("prob")
+        nc.scalar.activation(prob[:], p[:], ACT.Copy, scale=rz[:])
+        c_prob = wide("c_prob")
         c_mean = sb.tile([P, 1], F32, name="c_mean")
-        nc.vector.scalar_tensor_tensor(cp[:], c_ps[:], rz[:], p[:], ALU.mult, ALU.mult, accum_out=c_mean[:])
-        nc.vector.scalar_tensor_tensor(pg[:, 3, :], pg[:, 6, :], PEN, pg[:, 7, :], ALU.mult, ALU.mult)
+        nc.vector.scalar_tensor_tensor(c_prob[:], c_ps[:], rz[:], p[:], ALU.mult, ALU.mult, accum_out=c_mean[:])
+        nc.vector.scalar_tensor_tensor(coef[:, C1, :], coef[:, HV, :], K, coef[:, U, :], ALU.mult, ALU.mult)
+
         w = wide("w")
         wa = wide("wa")
         a_dot = sb.tile([P, PAGES], F32, name="a_dot")
         for h in range(HALVES):
-            nc.vector.scalar_tensor_tensor(w[:, cols(h)], c_ps[:, cols(h)], c_mean[:], pn[:, cols(h)], ALU.subtract, ALU.mult)
+            nc.vector.scalar_tensor_tensor(w[:, cols(h)], c_ps[:, cols(h)], c_mean[:], prob[:, cols(h)], ALU.subtract, ALU.mult)
         w_sq = wide("w_sq")
         nc.scalar.activation(w_sq[:], w[:], ACT.Square)
         for h in range(HALVES):
             nc.vector.tensor_tensor(wa[:, cols(h)], a_ps[h][:], w[:, cols(h)], ALU.mult)
         for h in range(HALVES):
             nc.vector.tensor_reduce(a_dot[:, pages(h)], by_page(wa[:, cols(h)]), AX.X, ALU.add)
-        nc.vector.tensor_reduce(nn[:, 1, 0:HP], by_page(w[:, cols(0)]), AX.X, ALU.add)
-        nc.vector.tensor_tensor(pg[:, 0:3, :], pg[:, 3:6, :], a_dot[:].unsqueeze(1).to_broadcast([P, 3, PAGES]), ALU.mult)
-        nc.vector.tensor_reduce(nn[:, 1, HP:PAGES], by_page(w[:, cols(1)]), AX.X, ALU.add)
-        c1b = sb.tile([P, PAGES], F32, name="c1b")
-        nc.vector.tensor_reduce(nn[:, 3, 0:HP], by_page(w_sq[:, cols(0)]), AX.X, ALU.add)
-        nc.vector.tensor_tensor(c1b[:], pg[:, 3, :], nn[:, 1, :], ALU.mult)
-        nc.vector.tensor_reduce(nn[:, 3, HP:PAGES], by_page(w_sq[:, cols(1)]), AX.X, ALU.add)
-        nc.vector.scalar_tensor_tensor(nn[:, 2, :], pg[:, 1, :], 16.0, c1b[:], ALU.mult, ALU.add)
+        for h in range(HALVES):
+            nc.vector.tensor_tensor(coef[:, BETA : TA + 1, pages(h)], coef[:, C1 : TQ + 1, pages(h)], a_dot[:, pages(h)].unsqueeze(1).to_broadcast([P, 3, HALF_PAGES]), ALU.mult)
+            nc.vector.tensor_reduce(sums[:, B, pages(h)], by_page(w[:, cols(h)]), AX.X, ALU.add)
+        c1_b = sb.tile([P, PAGES], F32, name="c1_b")
+        nc.vector.tensor_reduce(sums[:, W, pages(0)], by_page(w_sq[:, cols(0)]), AX.X, ALU.add)
+        nc.vector.tensor_tensor(c1_b[:], coef[:, C1, :], sums[:, B, :], ALU.mult)
+        nc.vector.tensor_reduce(sums[:, W, pages(1)], by_page(w_sq[:, cols(1)]), AX.X, ALU.add)
+        nc.vector.scalar_tensor_tensor(sums[:, GAMMA, :], coef[:, C3A, :], float(PAGE), c1_b[:], ALU.mult, ALU.add)
 
-        f1 = wide("f1")
+        f_w = wide("f_w")
         for g in range(PAGES):
-            sl = slice(g * PAGE, (g + 1) * PAGE)
-            nc.scalar.activation(f1[:, sl], w[:, sl], ACT.Identity, scale=alpha[:, g : g + 1], bias=pg[:, 0, g : g + 1])
+            nc.scalar.activation(f_w[:, page_cols(g)], w[:, page_cols(g)], ACT.Identity, scale=alpha[:, g : g + 1], bias=coef[:, BETA, g : g + 1])
 
-        ga = wide("ga")
+        f_a = wide("f_a")
         f = wide("f")
         terms = sb.tile([P, 3, PAGES], F32, name="terms")
-        nc.vector.tensor_tensor(by_page(ga[:, cols(0)]), by_page(a_ps[0][:]), spread(nn[:, 2, pages(0)]), ALU.mult)
-        nc.vector.tensor_tensor(terms[:], pg[:, 1:4, :], nn[:, 1:4, :], ALU.mult)
-        nc.vector.tensor_tensor(by_page(ga[:, cols(1)]), by_page(a_ps[1][:]), spread(nn[:, 2, pages(1)]), ALU.mult)
-        nc.vector.tensor_reduce(nn[:, 0, :], terms[:].rearrange("p r g -> p g r"), AX.X, ALU.add)
+        nc.vector.tensor_tensor(by_page(f_a[:, cols(0)]), by_page(a_ps[0][:]), spread(sums[:, GAMMA, pages(0)]), ALU.mult)
+        nc.vector.tensor_tensor(terms[:], coef[:, C3A : C1 + 1, :], sums[:, B : W + 1, :], ALU.mult)
+        nc.vector.tensor_tensor(by_page(f_a[:, cols(1)]), by_page(a_ps[1][:]), spread(sums[:, GAMMA, pages(1)]), ALU.mult)
+        nc.vector.tensor_reduce(sums[:, REST, :], terms[:].rearrange("p r g -> p g r"), AX.X, ALU.add)
         for h in range(HALVES):
-            nc.vector.tensor_tensor(f[:, cols(h)], f1[:, cols(h)], ga[:, cols(h)], ALU.add)
+            nc.vector.tensor_tensor(f[:, cols(h)], f_w[:, cols(h)], f_a[:, cols(h)], ALU.add)
+
         fw = wide("fw")
-        fp = wide("fp")
-        h1 = sb.tile([P, 1], F32, name="h1")
-        neg_h0 = sb.tile([P, 1], F32, name="neg_h0")
-        y = wide("y")
+        neg_f_prob = wide("neg_f_prob")
+        fw_sum = sb.tile([P, 1], F32, name="fw_sum")
+        neg_f_mean = sb.tile([P, 1], F32, name="neg_f_mean")
+        direct = wide("direct")
         for g in range(PAGES):
-            sl = slice(g * PAGE, (g + 1) * PAGE)
-            nc.scalar.activation(y[:, sl], w[:, sl], ACT.Identity, scale=nn[:, 2, g : g + 1], bias=nn[:, 0, g : g + 1])
-        z0 = wide("z0")
-        nc.vector.scalar_tensor_tensor(fp[:], f[:], -1.0, pn[:], ALU.mult, ALU.mult, accum_out=neg_h0[:])
-        nc.vector.tensor_tensor(z0[:, cols(0)], base_sb[:, cols(0)], y[:, cols(0)], ALU.add)
-        nc.vector.scalar_tensor_tensor(fw[:], f[:], neg_h0[:], w[:], ALU.add, ALU.mult, accum_out=h1[:])
-        nc.vector.tensor_tensor(z0[:, cols(1)], base_sb[:, cols(1)], y[:, cols(1)], ALU.add)
+            nc.scalar.activation(direct[:, page_cols(g)], w[:, page_cols(g)], ACT.Identity, scale=sums[:, GAMMA, g : g + 1], bias=sums[:, REST, g : g + 1])
+        with_base = wide("with_base")
+        nc.vector.scalar_tensor_tensor(neg_f_prob[:], f[:], -1.0, prob[:], ALU.mult, ALU.mult, accum_out=neg_f_mean[:])
+        nc.vector.tensor_tensor(with_base[:, cols(0)], base_sb[:, cols(0)], direct[:, cols(0)], ALU.add)
+        nc.vector.scalar_tensor_tensor(fw[:], f[:], neg_f_mean[:], w[:], ALU.add, ALU.mult, accum_out=fw_sum[:])
+        nc.vector.tensor_tensor(with_base[:, cols(1)], base_sb[:, cols(1)], direct[:, cols(1)], ALU.add)
         neg_hs = wide("neg_hs")
         for h in range(HALVES):
-            nc.vector.scalar_tensor_tensor(neg_hs[:, cols(h)], pn[:, cols(h)], h1[:], fw[:, cols(h)], ALU.mult, ALU.subtract)
-        uh = wide("uh")
+            nc.vector.scalar_tensor_tensor(neg_hs[:, cols(h)], prob[:, cols(h)], fw_sum[:], fw[:, cols(h)], ALU.mult, ALU.subtract)
+
+        neg_u_hs = wide("neg_u_hs")
         for g in range(PAGES):
-            sl = slice(g * PAGE, (g + 1) * PAGE)
-            nc.scalar.activation(uh[:, sl], neg_hs[:, sl], ACT.Copy, scale=pg[:, 7, g : g + 1])
-        hsa = wide("hsa")
-        neg_s = sb.tile([P, PAGES], F32, name="neg_s")
-        x = sb.tile([P, PAGES], F32, name="x")
+            nc.scalar.activation(neg_u_hs[:, page_cols(g)], neg_hs[:, page_cols(g)], ACT.Copy, scale=coef[:, U, g : g + 1])
+        neg_hs_a = wide("neg_hs_a")
+        neg_hs_dot = sb.tile([P, PAGES], F32, name="neg_hs_dot")
+        neg_page_term = sb.tile([P, PAGES], F32, name="neg_page_term")
         for h in range(HALVES):
-            nc.vector.tensor_tensor(hsa[:, cols(h)], a_ps[h][:], neg_hs[:, cols(h)], ALU.mult)
+            nc.vector.tensor_tensor(neg_hs_a[:, cols(h)], a_ps[h][:], neg_hs[:, cols(h)], ALU.mult)
         for h in range(HALVES):
-            nc.vector.tensor_reduce(neg_s[:, pages(h)], by_page(hsa[:, cols(h)]), AX.X, ALU.add)
-        z1 = wide("z1")
-        res = wide("res")
-        nc.vector.tensor_tensor(z1[:, cols(0)], z0[:, cols(0)], uh[:, cols(0)], ALU.subtract)
-        nc.vector.tensor_tensor(x[:], neg_s[:], pg[:, 6, :], ALU.mult)
-        nc.vector.tensor_tensor(z1[:, cols(1)], z0[:, cols(1)], uh[:, cols(1)], ALU.subtract)
+            nc.vector.tensor_reduce(neg_hs_dot[:, pages(h)], by_page(neg_hs_a[:, cols(h)]), AX.X, ALU.add)
+        with_hs = wide("with_hs")
+        result = wide("result")
+        nc.vector.tensor_tensor(with_hs[:, cols(0)], with_base[:, cols(0)], neg_u_hs[:, cols(0)], ALU.subtract)
+        nc.vector.tensor_tensor(neg_page_term[:], neg_hs_dot[:], coef[:, HV, :], ALU.mult)
+        nc.vector.tensor_tensor(with_hs[:, cols(1)], with_base[:, cols(1)], neg_u_hs[:, cols(1)], ALU.subtract)
         for h in range(HALVES):
-            nc.vector.tensor_tensor(by_page(res[:, cols(h)]), by_page(z1[:, cols(h)]), spread(x[:, pages(h)]), ALU.subtract)
-            nc.sync.dma_start(out=out[:, cols(h)], in_=res[:, cols(h)])
+            nc.vector.tensor_tensor(by_page(result[:, cols(h)]), by_page(with_hs[:, cols(h)]), spread(neg_page_term[:, pages(h)]), ALU.subtract)
+            nc.sync.dma_start(out=out[:, cols(h)], in_=result[:, cols(h)])

import math
from contextlib import ExitStack

import concourse.mybir as mybir

DEPTH, TOKENS, SLOTS, ROWS = 512, 2048, 512, 128
PAGES, PAGE = 32, 16
FLOPS = 2 * 2 * DEPTH * ROWS * SLOTS
P = 128
PACK = 4
SCALE_ROWS = DEPTH // 32
HALVES = 2
HALF_SLOTS = SLOTS // HALVES
HALF_PAGES = PAGES // HALVES
K = 512.0 * 2.0 * 512.0

BETA, C3A, TA, C1, C3, TQ, HV, U = range(8)
REST, B, GAMMA, W = range(4)

F32 = mybir.dt.float32
BF16 = mybir.dt.bfloat16
I32 = mybir.dt.int32
U32 = mybir.dt.uint32
U16 = mybir.dt.uint16
U8 = mybir.dt.uint8
FP8X4 = mybir.dt.float8_e4m3fn_x4
FP4X4 = mybir.dt.float4_e2m1fn_x4
ALU = mybir.AluOpType
ACT = mybir.ActivationFunctionType
AX = mybir.AxisListType


def cols(half):
    return slice(half * HALF_SLOTS, (half + 1) * HALF_SLOTS)


def pages(half):
    return slice(half * HALF_PAGES, (half + 1) * HALF_PAGES)


def page_cols(page):
    return slice(page * PAGE, (page + 1) * PAGE)


def by_page(ap):
    return ap.rearrange("p (g j) -> p g j", j=PAGE)


def spread(ap):
    return ap.unsqueeze(2).to_broadcast([P, ap.shape[1], PAGE])


def tile_attend_gppagemates_kernel(tc, query, keys_words, keys_scales, helpf, gout, vals_words, vals_scales, base, offs, out):
    nc = tc.nc
    with ExitStack() as ctx:
        sb = ctx.enter_context(tc.tile_pool(name="sb", bufs=1))
        ps = ctx.enter_context(tc.psum_pool(name="ps", bufs=1))

        def wide(name):
            return sb.tile([P, SLOTS], F32, name=name, align_bytes=64)

        def load_scales(plane, scales):
            for r in range(4):
                nc.sync.dma_start(out=plane[:].bitcast(I32)[r:P:32, :], in_=scales[0].bitcast(I32)[r:SCALE_ROWS:4, :])

        def cast(raw, name):
            grouped = sb.tile([P, ROWS, PACK], BF16, name=name + "_bf", tag=name + "_bf", align_bytes=64)
            nc.scalar.copy(grouped[:], raw[:].rearrange("p j w -> p w j"))
            return grouped

        def quantise(grouped, name):
            codes = sb.tile([P, ROWS], U32, name=name + "_codes", align_bytes=64)
            plane = sb.tile([P, ROWS], U8, name=name + "_plane", align_bytes=64)
            nc.vector.quantize_mx(out=codes[:].bitcast(FP8X4), scales=plane[:], in_=grouped[:].rearrange("p w j -> p (w j)"))
            return codes, plane

        def gather(dst, window, listed):
            nc.vector.tensor_copy(dst, window[:].indirect(listed))

        def product(dst, codes, plane, words, words_plane):
            nc.tensor.matmul_mx(out=dst, lhsT=codes[:].bitcast(FP8X4), lhsT_scale=plane[:], rhs=words.bitcast(FP4X4), rhs_scale=words_plane, start=True, stop=True)

        offsets = sb.tile([P, SLOTS // 16], U16, name="offsets")
        k_words = sb.tile([P, TOKENS], U16, name="k_words", align_bytes=64)
        k_plane = sb.tile([P, TOKENS], U8, name="k_plane", align_bytes=64)
        v_plane = sb.tile([P, TOKENS], U8, name="v_plane", tag="v_plane", align_bytes=64)
        q_raw = sb.tile([P, PACK, ROWS], F32, name="q_raw", tag="q_raw", align_bytes=64)
        help_col = sb.tile([P, 1], F32, name="help_col")

        nc.vector.memset(k_plane[:].bitcast(I32), 0)
        nc.vector.memset(v_plane[:].bitcast(I32), 0)

        nc.sync.dma_start(out=k_words[:].bitcast(I32), in_=keys_words[0].bitcast(I32))
        nc.sync.dma_start(offsets[:], offs)
        nc.sync.dma_start(out=help_col[:], in_=helpf)
        load_scales(k_plane, keys_scales)
        nc.sync.dma_start(out=q_raw[:], in_=query.rearrange("(p j) w -> p j w", j=PACK))
        load_scales(v_plane, vals_scales)
        g_raw = sb.tile([P, PACK, ROWS], F32, name="g_raw", tag="g_raw", align_bytes=64)
        v_words = sb.tile([P, TOKENS], U16, name="v_words", tag="v_words", align_bytes=64)
        nc.sync.dma_start(out=g_raw[:], in_=gout.rearrange("(p j) w -> p j w", j=PACK))
        nc.sync.dma_start(out=v_words[:].bitcast(I32), in_=vals_words[0].bitcast(I32))
        base_sb = wide("base_sb")
        nc.sync.dma_start(out=base_sb[:], in_=base)

        row_fac = sb.tile([P, 4], F32, name="row_fac")
        for j, (times, plus) in enumerate(((0.5, 0.0), (0.5, 1.0), (-1.0 / 16, 0.0), (1.0 / 16, 0.0))):
            nc.scalar.activation(row_fac[:, j : j + 1], help_col[:], ACT.Copy, scale=times, bias=plus)

        kg_words = sb.tile([P, SLOTS], U16, name="kg_words", align_bytes=64)
        kg_plane = sb.tile([P, SLOTS], U8, name="kg_plane", align_bytes=64)
        vg_plane = sb.tile([P, SLOTS], U8, name="vg_plane", align_bytes=64)
        a_ps = [ps.tile([P, HALF_SLOTS], F32, name="a_ps%d" % h) for h in range(HALVES)]
        c_ps = ps.tile([P, SLOTS], F32, name="c_ps")

        q_bf = cast(q_raw, "q")
        g_bf = cast(g_raw, "g")
        gather(kg_words[:], k_words, offsets[:])
        gather(kg_plane[:], k_plane, offsets[:])
        q_codes, q_plane = quantise(q_bf, "q")
        for h in range(HALVES):
            product(a_ps[h][:], q_codes, q_plane, kg_words[:, cols(h)], kg_plane[:, cols(h)])

        gather(vg_plane[:], v_plane, offsets[:])
        coef = sb.tile([P, 8, PAGES], F32, name="coef")
        sums = sb.tile([P, 4, PAGES], F32, name="sums")
        a_sum = sb.tile([P, PAGES], F32, name="a_sum", tag="v_plane", align_bytes=64)
        th = sb.tile([P, PAGES], F32, name="th", tag="g_raw", align_bytes=64)
        for h in range(HALVES):
            nc.vector.tensor_reduce(a_sum[:, pages(h)], by_page(a_ps[h][:]), AX.X, ALU.add)
        for h in range(HALVES):
            nc.scalar.activation(th[:, pages(h)], a_sum[:, pages(h)], ACT.Tanh, scale=2.0 / PAGE)
            nc.scalar.activation(coef[:, U, pages(h)], th[:, pages(h)], ACT.Identity, scale=row_fac[:, 0:1], bias=row_fac[:, 1:2])
        g_codes, g_plane = quantise(g_bf, "g")
        vg_words0 = sb.tile([P, HALF_SLOTS], U16, name="vg_words0", align_bytes=64)
        gather(vg_words0[:], v_words, offsets[:, pages(0)])

        s = wide("s")
        for h in range(HALVES):
            nc.vector.tensor_tensor(by_page(s[:, cols(h)]), by_page(a_ps[h][:]), spread(coef[:, U, pages(h)]), ALU.mult)
        half_max = [sb.tile([P, 1], F32, name="half_max%d" % h, tag="half_max%d" % h, align_bytes=64) for h in range(HALVES)]
        for h in range(HALVES):
            nc.vector.tensor_reduce(half_max[h][:], s[:, cols(h)], AX.X, ALU.max, negate=True)
        neg_max = sb.tile([P, 1], F32, name="neg_max")
        nc.vector.tensor_tensor(neg_max[:], half_max[0][:], half_max[1][:], ALU.min)
        vg_words1 = sb.tile([P, HALF_SLOTS], U16, name="vg_words1", tag="half_max0", align_bytes=64)
        gather(vg_words1[:], v_words, offsets[:, pages(1)])
        for h, words in enumerate((vg_words0, vg_words1)):
            product(c_ps[:, cols(h)], g_codes, g_plane, words[:], vg_plane[:, cols(h)])

        p = wide("p")
        z = sb.tile([P, 1], F32, name="z")
        nc.scalar.activation(p[:], s[:], ACT.Exp, bias=neg_max[:], accum_out=z[:])
        th_sq = sb.tile([P, PAGES], F32, name="th_sq")
        alpha = sb.tile([P, PAGES], F32, name="alpha")
        nc.scalar.activation(th_sq[:], th[:], ACT.Square)
        nc.scalar.activation(coef[:, TQ, :], th[:], ACT.Copy, scale=-0.25)
        nc.scalar.activation(alpha[:], coef[:, U, :], ACT.Square, scale=math.sqrt(K))
        nc.scalar.activation(coef[:, HV, :], th_sq[:], ACT.Identity, scale=row_fac[:, 2:3], bias=row_fac[:, 3:4])
        nc.scalar.activation(coef[:, C3, :], coef[:, HV, :], ACT.Square, scale=math.sqrt(K))

        rz = sb.tile([P, 1], F32, name="rz", tag="v_words", align_bytes=64)
        nc.vector.reciprocal(rz[:], z[:])
        prob = wide("prob")
        nc.scalar.activation(prob[:], p[:], ACT.Copy, scale=rz[:])
        c_prob = wide("c_prob")
        c_mean = sb.tile([P, 1], F32, name="c_mean")
        nc.vector.scalar_tensor_tensor(c_prob[:], c_ps[:], rz[:], p[:], ALU.mult, ALU.mult, accum_out=c_mean[:])
        nc.vector.scalar_tensor_tensor(coef[:, C1, :], coef[:, HV, :], K, coef[:, U, :], ALU.mult, ALU.mult)

        w = wide("w")
        wa = wide("wa")
        a_dot = sb.tile([P, PAGES], F32, name="a_dot")
        for h in range(HALVES):
            nc.vector.scalar_tensor_tensor(w[:, cols(h)], c_ps[:, cols(h)], c_mean[:], prob[:, cols(h)], ALU.subtract, ALU.mult)
        w_sq = wide("w_sq")
        nc.scalar.activation(w_sq[:], w[:], ACT.Square)
        for h in range(HALVES):
            nc.vector.tensor_tensor(wa[:, cols(h)], a_ps[h][:], w[:, cols(h)], ALU.mult)
        for h in range(HALVES):
            nc.vector.tensor_reduce(a_dot[:, pages(h)], by_page(wa[:, cols(h)]), AX.X, ALU.add)
        for h in range(HALVES):
            nc.vector.tensor_tensor(coef[:, BETA : TA + 1, pages(h)], coef[:, C1 : TQ + 1, pages(h)], a_dot[:, pages(h)].unsqueeze(1).to_broadcast([P, 3, HALF_PAGES]), ALU.mult)
            nc.vector.tensor_reduce(sums[:, B, pages(h)], by_page(w[:, cols(h)]), AX.X, ALU.add)
        c1_b = sb.tile([P, PAGES], F32, name="c1_b")
        nc.vector.tensor_reduce(sums[:, W, pages(0)], by_page(w_sq[:, cols(0)]), AX.X, ALU.add)
        nc.vector.tensor_tensor(c1_b[:], coef[:, C1, :], sums[:, B, :], ALU.mult)
        nc.vector.tensor_reduce(sums[:, W, pages(1)], by_page(w_sq[:, cols(1)]), AX.X, ALU.add)
        nc.vector.scalar_tensor_tensor(sums[:, GAMMA, :], coef[:, C3A, :], float(PAGE), c1_b[:], ALU.mult, ALU.add)

        f_w = wide("f_w")
        for g in range(PAGES):
            nc.scalar.activation(f_w[:, page_cols(g)], w[:, page_cols(g)], ACT.Identity, scale=alpha[:, g : g + 1], bias=coef[:, BETA, g : g + 1])

        f_a = wide("f_a")
        f = wide("f")
        terms = sb.tile([P, 3, PAGES], F32, name="terms")
        nc.vector.tensor_tensor(by_page(f_a[:, cols(0)]), by_page(a_ps[0][:]), spread(sums[:, GAMMA, pages(0)]), ALU.mult)
        nc.vector.tensor_tensor(terms[:], coef[:, C3A : C1 + 1, :], sums[:, B : W + 1, :], ALU.mult)
        nc.vector.tensor_tensor(by_page(f_a[:, cols(1)]), by_page(a_ps[1][:]), spread(sums[:, GAMMA, pages(1)]), ALU.mult)
        nc.vector.tensor_reduce(sums[:, REST, :], terms[:].rearrange("p r g -> p g r"), AX.X, ALU.add)
        for h in range(HALVES):
            nc.vector.tensor_tensor(f[:, cols(h)], f_w[:, cols(h)], f_a[:, cols(h)], ALU.add)

        fw = wide("fw")
        neg_f_prob = wide("neg_f_prob")
        fw_sum = sb.tile([P, 1], F32, name="fw_sum")
        neg_f_mean = sb.tile([P, 1], F32, name="neg_f_mean")
        direct = wide("direct")
        for g in range(PAGES):
            nc.scalar.activation(direct[:, page_cols(g)], w[:, page_cols(g)], ACT.Identity, scale=sums[:, GAMMA, g : g + 1], bias=sums[:, REST, g : g + 1])
        with_base = wide("with_base")
        nc.vector.scalar_tensor_tensor(neg_f_prob[:], f[:], -1.0, prob[:], ALU.mult, ALU.mult, accum_out=neg_f_mean[:])
        nc.vector.tensor_tensor(with_base[:, cols(0)], base_sb[:, cols(0)], direct[:, cols(0)], ALU.add)
        nc.vector.scalar_tensor_tensor(fw[:], f[:], neg_f_mean[:], w[:], ALU.add, ALU.mult, accum_out=fw_sum[:])
        nc.vector.tensor_tensor(with_base[:, cols(1)], base_sb[:, cols(1)], direct[:, cols(1)], ALU.add)
        neg_hs = wide("neg_hs")
        for h in range(HALVES):
            nc.vector.scalar_tensor_tensor(neg_hs[:, cols(h)], prob[:, cols(h)], fw_sum[:], fw[:, cols(h)], ALU.mult, ALU.subtract)

        neg_u_hs = wide("neg_u_hs")
        for g in range(PAGES):
            nc.scalar.activation(neg_u_hs[:, page_cols(g)], neg_hs[:, page_cols(g)], ACT.Copy, scale=coef[:, U, g : g + 1])
        neg_hs_a = wide("neg_hs_a")
        neg_hs_dot = sb.tile([P, PAGES], F32, name="neg_hs_dot")
        neg_page_term = sb.tile([P, PAGES], F32, name="neg_page_term")
        for h in range(HALVES):
            nc.vector.tensor_tensor(neg_hs_a[:, cols(h)], a_ps[h][:], neg_hs[:, cols(h)], ALU.mult)
        for h in range(HALVES):
            nc.vector.tensor_reduce(neg_hs_dot[:, pages(h)], by_page(neg_hs_a[:, cols(h)]), AX.X, ALU.add)
        with_hs = wide("with_hs")
        result = wide("result")
        nc.vector.tensor_tensor(with_hs[:, cols(0)], with_base[:, cols(0)], neg_u_hs[:, cols(0)], ALU.subtract)
        nc.vector.tensor_tensor(neg_page_term[:], neg_hs_dot[:], coef[:, HV, :], ALU.mult)
        nc.vector.tensor_tensor(with_hs[:, cols(1)], with_base[:, cols(1)], neg_u_hs[:, cols(1)], ALU.subtract)
        for h in range(HALVES):
            nc.vector.tensor_tensor(by_page(result[:, cols(h)]), by_page(with_hs[:, cols(h)]), spread(neg_page_term[:, pages(h)]), ALU.subtract)
            nc.sync.dma_start(out=out[:, cols(h)], in_=result[:, cols(h)])
